import numpy as np
import ml_dtypes


def mxq(x, axis, fmt="e4m3"):
    dtype, down = {"e4m3": (ml_dtypes.float8_e4m3fn, 7), "e5m2": (ml_dtypes.float8_e5m2, 14)}[fmt]
    v = np.moveaxis(np.asarray(x, np.float32).astype(ml_dtypes.bfloat16).astype(np.float64), axis, -1)
    blocks = v.reshape(v.shape[:-1] + (-1, 32))
    amax = np.abs(blocks).max(-1, keepdims=True)
    byte = np.maximum(np.where(amax > 0, np.frexp(amax)[1] - 1 + 127, 0) - down, 1)
    scale = np.exp2(byte - 127.0)
    codes = (blocks / scale).astype(np.float32).astype(dtype).astype(np.float64)
    return np.moveaxis((codes * scale).reshape(v.shape), -1, axis)


WIDE = False


def mx_kscale(k):
    if not WIDE:
        return np.ones(k)
    levels = np.array([10, -10, 5, -5, 0])
    if k % 512:
        return np.exp2(np.random.permutation(np.resize(levels, k // 32))).repeat(32)
    a = np.empty((k // 512, 16))
    for p in range(k // 512):
        a[p, :8] = np.random.permutation(np.resize(levels, 8))
        for g in range(8):
            far = levels[np.abs(levels - a[p, g]) >= 10]
            a[p, g + 8] = far[np.random.randint(len(far))]
    return np.exp2(a.ravel()).repeat(32)


def f64(x):
    return np.asarray(x).astype(np.float64)


def striped8(idx):
    return np.asarray(idx).reshape(8, -1, 16).transpose(0, 2, 1).reshape(128, -1).astype(np.uint16)


def unstriped8(offs):
    return offs.reshape(8, 16, -1).transpose(0, 2, 1).reshape(8, -1).astype(np.int64)


def pick8(x, idx, run):
    r = np.arange(len(x))
    return x[r[:, None], idx[r % (8 * run) // run]]


E2M1 = np.array([0.0, 0.5, 1.0, 1.5, 2.0, 3.0, 4.0, 6.0, -0.0, -0.5, -1.0, -1.5, -2.0, -3.0, -4.0, -6.0])


def pack_weight(w, fmt):
    k, n = w.shape
    w = f64(np.asarray(w, np.float32).astype(ml_dtypes.bfloat16)).reshape(k // 32, 32, n)
    amax = np.abs(w).max(1)
    if fmt == "e4m3":
        byte = np.frexp(amax)[1] - 1 + 127 - 7
    else:
        mant, ex = np.frexp(amax / 6.0)
        byte = np.where(mant > 0.5, ex, ex - 1) + 127
    byte = np.clip(np.where(amax > 0, byte, 1), 1, 254)
    scaled = (w * np.exp2(127.0 - byte)[:, None, :]).reshape(k, n).astype(np.float32)
    by_word = np.ascontiguousarray(scaled.reshape(k // 512, 128, 4, n).transpose(0, 1, 3, 2))
    if fmt == "e4m3":
        words = by_word.astype(ml_dtypes.float8_e4m3fn).view(np.uint8)
    else:
        c = by_word.astype(ml_dtypes.float4_e2m1fn).view(np.uint8) & 0xF
        words = (c[..., 0::2] | (c[..., 1::2] << 4)).reshape(k // 512, 128, 2 * n)
    return np.ascontiguousarray(words), np.ascontiguousarray(byte.astype(np.uint8).reshape(k // 512, 16, n))


def unpack_weight(words, scales, fmt):
    g, _, n = scales.shape
    words = np.ascontiguousarray(words).reshape(g, 128, n, -1)
    if fmt == "e4m3":
        vals = words.view(ml_dtypes.float8_e4m3fn).astype(np.float64)
    else:
        nib = np.empty((g, 128, n, 4), np.uint8)
        nib[..., 0::2] = words & 0xF
        nib[..., 1::2] = words >> 4
        vals = E2M1[nib]
    vals = vals * np.repeat(np.exp2(scales.astype(np.float64) - 127.0), 8, axis=1)[..., None]
    return vals.transpose(0, 1, 3, 2).reshape(g * 512, n)


D, T, U, I, Q = 512, 1024, 1024, 512, 128


def setup_inputs():
    n = np.random.standard_normal
    idx = np.stack([np.random.permutation(T)[:I] for _ in range(8)])
    idx2 = np.stack([np.random.permutation(U)[:I] for _ in range(8)])
    idx3 = np.stack([np.random.permutation(U)[:I] for _ in range(8)])
    fd = mx_kscale(D)
    keysp = pack_weight(n((D, T)) / fd[:, None], "e2m1")
    notesp = pack_weight(n((D, U)) / fd[:, None], "e4m3")
    return {
        "query": (n((D, Q)) * 1.0 / np.sqrt(D) * fd[:, None]).astype(np.float32),
        "keys_words": keysp[0],
        "keys_scales": keysp[1],
        "notes_words": notesp[0],
        "notes_scales": notesp[1],
        "tau": (np.random.uniform(0.5, 1.5, (Q, 1))).astype(np.float32),
        "offs": striped8(idx),
        "offs2": striped8(idx2),
        "offs3": striped8(idx3),
    }


def reference(query, keys_words, keys_scales, notes_words, notes_scales, tau, offs, offs2, offs3):
    idx = unstriped8(offs)
    idx2 = unstriped8(offs2)
    idx3 = unstriped8(offs3)
    keysu = unpack_weight(keys_words, keys_scales, "e2m1")
    notesu = unpack_weight(notes_words, notes_scales, "e4m3")
    queryq = mxq(f64(query), 0, "e4m3")
    a = queryq.T @ keysu
    b = queryq.T @ notesu
    ta = np.max(a, axis=1, keepdims=True)
    bt = ta * f64(tau)
    e1 = np.exp(pick8(a, idx, 16) * f64(tau) - bt)
    f1 = np.zeros((Q, U))
    f1[np.arange(Q)[:, None], idx2[np.arange(Q) % 128 // 16]] = e1
    cc = b + f1 * 4.0
    y = pick8(cc, idx3, 16) - e1
    return y

@@ -1,0 +1,157 @@
+from contextlib import ExitStack
+
+import concourse.mybir as mybir
+
+D, T, U, I, Q = 512, 1024, 1024, 512, 128
+FLOPS = 2 * D * Q * (T + U)
+
+F32 = mybir.dt.float32
+BF16 = mybir.dt.bfloat16
+I32 = mybir.dt.int32
+U32 = mybir.dt.uint32
+U16 = mybir.dt.uint16
+U8 = mybir.dt.uint8
+FP8X4 = mybir.dt.float8_e4m3fn_x4
+FP4X4 = mybir.dt.float4_e2m1fn_x4
+ALU = mybir.AluOpType
+ACT = mybir.ActivationFunctionType
+
+P = 128
+PACK = 4
+BANK = 512
+HALF = I // 2
+LIST = 16
+CAST_SPLIT = 64
+CHUNK = 256
+POOL_COLS = 320
+
+
+def load_scales(queue, plane, scales):
+    for quad in range(4):
+        queue.dma_start(
+            out=plane[32 * quad : 32 * quad + 4, :].bitcast(I32),
+            in_=scales[0, 4 * quad : 4 * quad + 4, :].bitcast(I32),
+        )
+
+
+def tile_attend_temperedvotes_two_kernel(
+    tc, query, keys_words, keys_scales, notes_words, notes_scales, tau, offs, offs2, offs3, out
+):
+    nc = tc.nc
+    with ExitStack() as ctx:
+        lists = ctx.enter_context(tc.tile_pool(name="lists", bufs=1))
+        sb = ctx.enter_context(tc.tile_pool(name="sb", bufs=1))
+        psum = ctx.enter_context(tc.psum_pool(name="psum", bufs=1))
+
+        q_raw = sb.tile([P, PACK, Q], F32, tag="stage", align_bytes=64)
+        key_codes = sb.tile([P, 2 * T], U8, align_bytes=64)
+        key_plane = sb.tile([P, T], U8, align_bytes=64)
+        note_plane = sb.tile([P, U], U8, align_bytes=64)
+        temper = sb.tile([P, 1], F32)
+        pick_tokens = lists.tile([P, I // LIST], U16)
+        put_notes = lists.tile([P, I // LIST], U16)
+        pick_notes = lists.tile([P, I // LIST], U16)
+        votes = sb.tile([P, U], F32, align_bytes=64)
+
+        nc.vector.memset(key_plane[:].bitcast(I32), 0)
+        nc.vector.memset(note_plane[:].bitcast(I32), 0)
+        nc.vector.memset(votes[:], 0.0)
+        fours = sb.tile([P, HALF], F32, align_bytes=64)
+        nc.vector.memset(fours[:], 4.0)
+
+        nc.sync.dma_start(out=q_raw[:], in_=query.rearrange("(p j) q -> p j q", j=PACK))
+        nc.sync.dma_start(out=key_codes[:].bitcast(I32), in_=keys_words[0].bitcast(I32))
+        load_scales(nc.sync, key_plane, keys_scales)
+        nc.sync.dma_start(out=temper[:], in_=tau)
+        nc.sync.dma_start(pick_tokens[:], offs)
+
+        q_bf = sb.tile([P, Q, PACK], BF16, align_bytes=64)
+        q_turned = q_raw[:].rearrange("p j q -> p q j")
+        nc.vector.tensor_copy(out=q_bf[:, :CAST_SPLIT, :], in_=q_turned[:, :CAST_SPLIT, :])
+        nc.scalar.activation(q_bf[:, CAST_SPLIT:, :], q_turned[:, CAST_SPLIT:, :], ACT.Copy)
+
+        note_codes = sb.tile([P, U], I32, tag="stage", align_bytes=64)
+        nc.sync.dma_start(
+            out=note_codes[:], in_=notes_words[0].rearrange("p n t -> p (n t)").bitcast(I32)
+        )
+        nc.sync.dma_start(put_notes[:], offs2)
+        load_scales(nc.sync, note_plane, notes_scales)
+        nc.sync.dma_start(pick_notes[:], offs3)
+        q_codes = sb.tile([P, Q], U32, align_bytes=64)
+        q_plane = sb.tile([P, Q], U8, align_bytes=64)
+        nc.vector.quantize_mx(
+            out=q_codes[:].bitcast(FP8X4),
+            scales=q_plane[:],
+            in_=q_bf[:].rearrange("p q j -> p (q j)"),
+        )
+
+        neg_temper = sb.tile([P, 1], F32)
+        nc.vector.tensor_scalar(neg_temper[:], temper[:], -1.0, None, ALU.mult)
+
+        token_scores = sb.tile([P, T], F32, align_bytes=64)
+        tops = [sb.tile([P, 1], F32, name="top%d" % c) for c in range(4)]
+        for c in range(4):
+            cols = slice(c * CHUNK, (c + 1) * CHUNK)
+            bank = psum.tile([P, CHUNK], F32, name="token_bank%d" % c)
+            nc.tensor.matmul_mx(
+                out=bank[:],
+                lhsT=q_codes[:].bitcast(FP8X4),
+                lhsT_scale=q_plane[:],
+                rhs=key_codes[:, 2 * c * CHUNK : 2 * (c + 1) * CHUNK].bitcast(FP4X4),
+                rhs_scale=key_plane[:, cols],
+                start=True,
+                stop=True,
+            )
+            before = None if c < 2 else tops[c - 2][:]
+            nc.vector.tensor_scalar(
+                token_scores[:, cols], bank[:], 1.0, before, ALU.mult, ALU.max, accum_out=tops[c][:]
+            )
+        neg_bt = sb.tile([P, 1], F32)
+        nc.vector.tensor_scalar(neg_bt[:], tops[2][:], tops[3][:], neg_temper[:], ALU.max, ALU.mult)
+
+        note_banks = []
+        for h in range(2):
+            cols = slice(h * BANK, (h + 1) * BANK)
+            bank = psum.tile([P, BANK], F32, name="note_bank%d" % h)
+            nc.tensor.matmul_mx(
+                out=bank[:],
+                lhsT=q_codes[:].bitcast(FP8X4),
+                lhsT_scale=q_plane[:],
+                rhs=note_codes[:, cols].bitcast(FP8X4),
+                rhs_scale=note_plane[:, cols],
+                start=True,
+                stop=True,
+            )
+            note_banks.append(bank)
+
+        e1 = [sb.tile([P, HALF], F32, name="e1_%d" % h, align_bytes=64) for h in range(2)]
+        for h in range(2):
+            entries = slice(h * HALF // LIST, (h + 1) * HALF // LIST)
+            nc.scalar.activation(
+                e1[h][:],
+                token_scores[:].indirect(pick_tokens[:, entries]),
+                ACT.Exp,
+                bias=neg_bt[:],
+                scale=temper[:],
+            )
+            nc.vector.tensor_tensor(votes[:].indirect(put_notes[:, entries]), e1[h][:], fours[:], ALU.mult)
+
+        note_tail = sb.tile([P, POOL_COLS], F32, align_bytes=64)
+        nc.scalar.activation(note_tail[:], note_banks[1][:, BANK - POOL_COLS :], ACT.Copy)
+
+        cc = sb.tile([P, U], F32, align_bytes=64)
+        nc.gpsimd.tensor_tensor(cc[:, U - POOL_COLS :], votes[:, U - POOL_COLS :], note_tail[:], ALU.add)
+        nc.vector.tensor_tensor(cc[:, :BANK], votes[:, :BANK], note_banks[0][:], ALU.add)
+        nc.vector.tensor_tensor(
+            cc[:, BANK : U - POOL_COLS], votes[:, BANK : U - POOL_COLS], note_banks[1][:, : BANK - POOL_COLS], ALU.add
+        )
+
+        results = [sb.tile([P, HALF], F32, name="result%d" % h, align_bytes=64) for h in range(2)]
+        picked = sb.tile([P, HALF], F32, align_bytes=64)
+        nc.scalar.activation(picked[:], cc[:].indirect(pick_notes[:, HALF // LIST :]), ACT.Copy)
+        nc.vector.tensor_tensor(
+            results[0][:], cc[:].indirect(pick_notes[:, : HALF // LIST]), e1[0][:], ALU.subtract
+        )
+        nc.sync.dma_start(out=out[:, :HALF], in_=results[0][:])
+        nc.vector.tensor_tensor(results[1][:], picked[:], e1[1][:], ALU.subtract)
+        nc.sync.dma_start(out=out[:, HALF:], in_=results[1][:])

@@ -43,8 +43,9 @@ def tile_attend_temperedvotes_two_kernel(
         sb = ctx.enter_context(tc.tile_pool(name="sb", bufs=1))
         psum = ctx.enter_context(tc.psum_pool(name="psum", bufs=1))
 
-        q_raw = sb.tile([P, PACK, Q], F32, tag="stage", align_bytes=64)
-        key_codes = sb.tile([P, 2 * T], U8, align_bytes=64)
+        q_low = sb.tile([P, 2, Q], F32, align_bytes=64)
+        q_high = sb.tile([P, 2, Q], F32, tag="stage", align_bytes=64)
+        key_codes = [sb.tile([P, T], U8, name="key_codes%d" % h, align_bytes=64) for h in range(2)]
         key_plane = sb.tile([P, T], U8, align_bytes=64)
         note_plane = sb.tile([P, U], U8, align_bytes=64)
         temper = sb.tile([P, 1], F32)
@@ -59,22 +60,27 @@ def tile_attend_temperedvotes_two_kernel(
         fours = sb.tile([P, HALF], F32, align_bytes=64)
         nc.vector.memset(fours[:], 4.0)
 
-        nc.sync.dma_start(out=q_raw[:], in_=query.rearrange("(p j) q -> p j q", j=PACK))
-        nc.sync.dma_start(out=key_codes[:].bitcast(I32), in_=keys_words[0].bitcast(I32))
+        q_rows = query.rearrange("(p j) q -> p j q", j=PACK)
+        key_words = keys_words[0].bitcast(I32)
+        nc.sync.dma_start(out=q_low[:], in_=q_rows[:, :2, :])
+        nc.sync.dma_start(out=q_high[:], in_=q_rows[:, 2:, :])
+        nc.sync.dma_start(out=key_codes[0][:].bitcast(I32), in_=key_words[:, : T // 4])
         load_scales(nc.sync, key_plane, keys_scales)
+        nc.sync.dma_start(out=key_codes[1][:].bitcast(I32), in_=key_words[:, T // 4 :])
         nc.sync.dma_start(out=temper[:], in_=tau)
         nc.sync.dma_start(pick_tokens[:], offs)
+        nc.sync.dma_start(put_notes[:], offs2)
 
         q_bf = sb.tile([P, Q, PACK], BF16, align_bytes=64)
-        q_turned = q_raw[:].rearrange("p j q -> p q j")
-        nc.vector.tensor_copy(out=q_bf[:, :CAST_SPLIT, :], in_=q_turned[:, :CAST_SPLIT, :])
-        nc.scalar.activation(q_bf[:, CAST_SPLIT:, :], q_turned[:, CAST_SPLIT:, :], ACT.Copy)
+        nc.vector.tensor_copy(out=q_bf[:, :, :2], in_=q_low[:].rearrange("p j q -> p q j"))
+        high = q_high[:].rearrange("p j q -> p q j")
+        nc.vector.tensor_copy(out=q_bf[:, :CAST_SPLIT, 2:], in_=high[:, :CAST_SPLIT, :])
+        nc.scalar.activation(q_bf[:, CAST_SPLIT:, 2:], high[:, CAST_SPLIT:, :], ACT.Copy)
 
         note_codes = sb.tile([P, U], I32, tag="stage", align_bytes=64)
         nc.sync.dma_start(
             out=note_codes[:], in_=notes_words[0].rearrange("p n t -> p (n t)").bitcast(I32)
         )
-        nc.sync.dma_start(put_notes[:], offs2)
         load_scales(nc.sync, note_plane, notes_scales)
         nc.sync.dma_start(pick_notes[:], offs3)
         q_codes = sb.tile([P, Q], U32, align_bytes=64)
@@ -86,7 +92,7 @@ def tile_attend_temperedvotes_two_kernel(
         )
 
         neg_temper = sb.tile([P, 1], F32)
-        nc.vector.tensor_scalar(neg_temper[:], temper[:], -1.0, None, ALU.mult)
+        nc.scalar.activation(neg_temper[:], temper[:], ACT.Copy, scale=-1.0)
 
         token_scores = sb.tile([P, T], F32, align_bytes=64)
         tops = [sb.tile([P, 1], F32, name="top%d" % c) for c in range(4)]
@@ -97,15 +103,18 @@ def tile_attend_temperedvotes_two_kernel(
                 out=bank[:],
                 lhsT=q_codes[:].bitcast(FP8X4),
                 lhsT_scale=q_plane[:],
-                rhs=key_codes[:, 2 * c * CHUNK : 2 * (c + 1) * CHUNK].bitcast(FP4X4),
+                rhs=key_codes[c // 2][:, 2 * (c % 2) * CHUNK : 2 * (c % 2 + 1) * CHUNK].bitcast(FP4X4),
                 rhs_scale=key_plane[:, cols],
                 start=True,
                 stop=True,
             )
-            before = None if c < 2 else tops[c - 2][:]
-            nc.vector.tensor_scalar(
-                token_scores[:, cols], bank[:], 1.0, before, ALU.mult, ALU.max, accum_out=tops[c][:]
-            )
+            if c < 2:
+                nc.vector.tensor_reduce(tops[c][:], bank[:], mybir.AxisListType.X, ALU.max)
+                nc.scalar.activation(token_scores[:, cols], bank[:], ACT.Copy)
+            else:
+                nc.vector.tensor_scalar(
+                    token_scores[:, cols], bank[:], 1.0, tops[c - 2][:], ALU.mult, ALU.max, accum_out=tops[c][:]
+                )
         neg_bt = sb.tile([P, 1], F32)
         nc.vector.tensor_scalar(neg_bt[:], tops[2][:], tops[3][:], neg_temper[:], ALU.max, ALU.mult)
 
@@ -146,12 +155,15 @@ def tile_attend_temperedvotes_two_kernel(
             cc[:, BANK : U - POOL_COLS], votes[:, BANK : U - POOL_COLS], note_banks[1][:, : BANK - POOL_COLS], ALU.add
         )
 
-        results = [sb.tile([P, HALF], F32, name="result%d" % h, align_bytes=64) for h in range(2)]
+        first = sb.tile([P, HALF], F32, align_bytes=64)
         picked = sb.tile([P, HALF], F32, align_bytes=64)
         nc.scalar.activation(picked[:], cc[:].indirect(pick_notes[:, HALF // LIST :]), ACT.Copy)
         nc.vector.tensor_tensor(
-            results[0][:], cc[:].indirect(pick_notes[:, : HALF // LIST]), e1[0][:], ALU.subtract
+            first[:], cc[:].indirect(pick_notes[:, : HALF // LIST]), e1[0][:], ALU.subtract
         )
-        nc.sync.dma_start(out=out[:, :HALF], in_=results[0][:])
-        nc.vector.tensor_tensor(results[1][:], picked[:], e1[1][:], ALU.subtract)
-        nc.sync.dma_start(out=out[:, HALF:], in_=results[1][:])
+        nc.sync.dma_start(out=out[:, :HALF], in_=first[:])
+        for part in range(2):
+            cols = slice(part * HALF // 2, (part + 1) * HALF // 2)
+            last = sb.tile([P, HALF // 2], F32, name="last%d" % part, align_bytes=64)
+            nc.vector.tensor_tensor(last[:], picked[:, cols], e1[1][:, cols], ALU.subtract)
+            nc.sync.dma_start(out=out[:, HALF + cols.start : HALF + cols.stop], in_=last[:])

@@ -72,10 +72,10 @@ def tile_attend_temperedvotes_two_kernel(
         nc.sync.dma_start(put_notes[:], offs2)
 
         q_bf = sb.tile([P, Q, PACK], BF16, align_bytes=64)
-        nc.vector.tensor_copy(out=q_bf[:, :, :2], in_=q_low[:].rearrange("p j q -> p q j"))
-        high = q_high[:].rearrange("p j q -> p q j")
-        nc.vector.tensor_copy(out=q_bf[:, :CAST_SPLIT, 2:], in_=high[:, :CAST_SPLIT, :])
-        nc.scalar.activation(q_bf[:, CAST_SPLIT:, 2:], high[:, CAST_SPLIT:, :], ACT.Copy)
+        for pair, rows in ((slice(0, 2), q_low), (slice(2, 4), q_high)):
+            turned = rows[:].rearrange("p j q -> p q j")
+            nc.vector.tensor_copy(out=q_bf[:, :CAST_SPLIT, pair], in_=turned[:, :CAST_SPLIT, :])
+            nc.scalar.activation(q_bf[:, CAST_SPLIT:, pair], turned[:, CAST_SPLIT:, :], ACT.Copy)
 
         note_codes = sb.tile([P, U], I32, tag="stage", align_bytes=64)
         nc.sync.dma_start(
@@ -85,11 +85,12 @@ def tile_attend_temperedvotes_two_kernel(
         nc.sync.dma_start(pick_notes[:], offs3)
         q_codes = sb.tile([P, Q], U32, align_bytes=64)
         q_plane = sb.tile([P, Q], U8, align_bytes=64)
-        nc.vector.quantize_mx(
-            out=q_codes[:].bitcast(FP8X4),
-            scales=q_plane[:],
-            in_=q_bf[:].rearrange("p q j -> p (q j)"),
-        )
+        for rows in (slice(0, CAST_SPLIT), slice(CAST_SPLIT, Q)):
+            nc.vector.quantize_mx(
+                out=q_codes[:, rows].bitcast(FP8X4),
+                scales=q_plane[:, rows],
+                in_=q_bf[:, rows, :].rearrange("p q j -> p (q j)"),
+            )
 
         neg_temper = sb.tile([P, 1], F32)
         nc.scalar.activation(neg_temper[:], temper[:], ACT.Copy, scale=-1.0)

from contextlib import ExitStack

import concourse.mybir as mybir

D, T, U, I, Q = 512, 1024, 1024, 512, 128
FLOPS = 2 * D * Q * (T + U)

F32 = mybir.dt.float32
BF16 = mybir.dt.bfloat16
I32 = mybir.dt.int32
U32 = mybir.dt.uint32
U16 = mybir.dt.uint16
U8 = mybir.dt.uint8
FP8X4 = mybir.dt.float8_e4m3fn_x4
FP4X4 = mybir.dt.float4_e2m1fn_x4
ALU = mybir.AluOpType
ACT = mybir.ActivationFunctionType

P = 128
PACK = 4
BANK = 512
HALF = I // 2
LIST = 16
CAST_SPLIT = 64
CHUNK = 256
POOL_COLS = 320


def load_scales(queue, plane, scales):
    for quad in range(4):
        queue.dma_start(
            out=plane[32 * quad : 32 * quad + 4, :].bitcast(I32),
            in_=scales[0, 4 * quad : 4 * quad + 4, :].bitcast(I32),
        )


def tile_attend_temperedvotes_two_kernel(
    tc, query, keys_words, keys_scales, notes_words, notes_scales, tau, offs, offs2, offs3, out
):
    nc = tc.nc
    with ExitStack() as ctx:
        lists = ctx.enter_context(tc.tile_pool(name="lists", bufs=1))
        sb = ctx.enter_context(tc.tile_pool(name="sb", bufs=1))
        psum = ctx.enter_context(tc.psum_pool(name="psum", bufs=1))

        q_low = sb.tile([P, 2, Q], F32, align_bytes=64)
        q_high = sb.tile([P, 2, Q], F32, tag="stage", align_bytes=64)
        key_codes = [sb.tile([P, T], U8, name="key_codes%d" % h, align_bytes=64) for h in range(2)]
        key_plane = sb.tile([P, T], U8, align_bytes=64)
        note_plane = sb.tile([P, U], U8, align_bytes=64)
        temper = sb.tile([P, 1], F32)
        pick_tokens = lists.tile([P, I // LIST], U16)
        put_notes = lists.tile([P, I // LIST], U16)
        pick_notes = lists.tile([P, I // LIST], U16)
        votes = sb.tile([P, U], F32, align_bytes=64)

        nc.vector.memset(key_plane[:].bitcast(I32), 0)
        nc.vector.memset(note_plane[:].bitcast(I32), 0)
        nc.vector.memset(votes[:], 0.0)
        fours = sb.tile([P, HALF], F32, align_bytes=64)
        nc.vector.memset(fours[:], 4.0)

        q_rows = query.rearrange("(p j) q -> p j q", j=PACK)
        key_words = keys_words[0].bitcast(I32)
        nc.sync.dma_start(out=q_low[:], in_=q_rows[:, :2, :])
        nc.sync.dma_start(out=q_high[:], in_=q_rows[:, 2:, :])
        nc.sync.dma_start(out=key_codes[0][:].bitcast(I32), in_=key_words[:, : T // 4])
        load_scales(nc.sync, key_plane, keys_scales)
        nc.sync.dma_start(out=key_codes[1][:].bitcast(I32), in_=key_words[:, T // 4 :])
        nc.sync.dma_start(out=temper[:], in_=tau)
        nc.sync.dma_start(pick_tokens[:], offs)
        nc.sync.dma_start(put_notes[:], offs2)

        q_bf = sb.tile([P, Q, PACK], BF16, align_bytes=64)
        for pair, rows in ((slice(0, 2), q_low), (slice(2, 4), q_high)):
            turned = rows[:].rearrange("p j q -> p q j")
            nc.vector.tensor_copy(out=q_bf[:, :CAST_SPLIT, pair], in_=turned[:, :CAST_SPLIT, :])
            nc.scalar.activation(q_bf[:, CAST_SPLIT:, pair], turned[:, CAST_SPLIT:, :], ACT.Copy)

        note_codes = sb.tile([P, U], I32, tag="stage", align_bytes=64)
        nc.sync.dma_start(
            out=note_codes[:], in_=notes_words[0].rearrange("p n t -> p (n t)").bitcast(I32)
        )
        load_scales(nc.sync, note_plane, notes_scales)
        nc.sync.dma_start(pick_notes[:], offs3)
        q_codes = sb.tile([P, Q], U32, align_bytes=64)
        q_plane = sb.tile([P, Q], U8, align_bytes=64)
        for rows in (slice(0, CAST_SPLIT), slice(CAST_SPLIT, Q)):
            nc.vector.quantize_mx(
                out=q_codes[:, rows].bitcast(FP8X4),
                scales=q_plane[:, rows],
                in_=q_bf[:, rows, :].rearrange("p q j -> p (q j)"),
            )

        neg_temper = sb.tile([P, 1], F32)
        nc.scalar.activation(neg_temper[:], temper[:], ACT.Copy, scale=-1.0)

        token_scores = sb.tile([P, T], F32, align_bytes=64)
        tops = [sb.tile([P, 1], F32, name="top%d" % c) for c in range(4)]
        for c in range(4):
            cols = slice(c * CHUNK, (c + 1) * CHUNK)
            bank = psum.tile([P, CHUNK], F32, name="token_bank%d" % c)
            nc.tensor.matmul_mx(
                out=bank[:],
                lhsT=q_codes[:].bitcast(FP8X4),
                lhsT_scale=q_plane[:],
                rhs=key_codes[c // 2][:, 2 * (c % 2) * CHUNK : 2 * (c % 2 + 1) * CHUNK].bitcast(FP4X4),
                rhs_scale=key_plane[:, cols],
                start=True,
                stop=True,
            )
            if c < 2:
                nc.vector.tensor_reduce(tops[c][:], bank[:], mybir.AxisListType.X, ALU.max)
                nc.scalar.activation(token_scores[:, cols], bank[:], ACT.Copy)
            else:
                nc.vector.tensor_scalar(
                    token_scores[:, cols], bank[:], 1.0, tops[c - 2][:], ALU.mult, ALU.max, accum_out=tops[c][:]
                )
        neg_bt = sb.tile([P, 1], F32)
        nc.vector.tensor_scalar(neg_bt[:], tops[2][:], tops[3][:], neg_temper[:], ALU.max, ALU.mult)

        note_banks = []
        for h in range(2):
            cols = slice(h * BANK, (h + 1) * BANK)
            bank = psum.tile([P, BANK], F32, name="note_bank%d" % h)
            nc.tensor.matmul_mx(
                out=bank[:],
                lhsT=q_codes[:].bitcast(FP8X4),
                lhsT_scale=q_plane[:],
                rhs=note_codes[:, cols].bitcast(FP8X4),
                rhs_scale=note_plane[:, cols],
                start=True,
                stop=True,
            )
            note_banks.append(bank)

        e1 = [sb.tile([P, HALF], F32, name="e1_%d" % h, align_bytes=64) for h in range(2)]
        for h in range(2):
            entries = slice(h * HALF // LIST, (h + 1) * HALF // LIST)
            nc.scalar.activation(
                e1[h][:],
                token_scores[:].indirect(pick_tokens[:, entries]),
                ACT.Exp,
                bias=neg_bt[:],
                scale=temper[:],
            )
            nc.vector.tensor_tensor(votes[:].indirect(put_notes[:, entries]), e1[h][:], fours[:], ALU.mult)

        note_tail = sb.tile([P, POOL_COLS], F32, align_bytes=64)
        nc.scalar.activation(note_tail[:], note_banks[1][:, BANK - POOL_COLS :], ACT.Copy)

        cc = sb.tile([P, U], F32, align_bytes=64)
        nc.gpsimd.tensor_tensor(cc[:, U - POOL_COLS :], votes[:, U - POOL_COLS :], note_tail[:], ALU.add)
        nc.vector.tensor_tensor(cc[:, :BANK], votes[:, :BANK], note_banks[0][:], ALU.add)
        nc.vector.tensor_tensor(
            cc[:, BANK : U - POOL_COLS], votes[:, BANK : U - POOL_COLS], note_banks[1][:, : BANK - POOL_COLS], ALU.add
        )

        first = sb.tile([P, HALF], F32, align_bytes=64)
        picked = sb.tile([P, HALF], F32, align_bytes=64)
        nc.scalar.activation(picked[:], cc[:].indirect(pick_notes[:, HALF // LIST :]), ACT.Copy)
        nc.vector.tensor_tensor(
            first[:], cc[:].indirect(pick_notes[:, : HALF // LIST]), e1[0][:], ALU.subtract
        )
        nc.sync.dma_start(out=out[:, :HALF], in_=first[:])
        for part in range(2):
            cols = slice(part * HALF // 2, (part + 1) * HALF // 2)
            last = sb.tile([P, HALF // 2], F32, name="last%d" % part, align_bytes=64)
            nc.vector.tensor_tensor(last[:], picked[:, cols], e1[1][:, cols], ALU.subtract)
            nc.sync.dma_start(out=out[:, HALF + cols.start : HALF + cols.stop], in_=last[:])
